import numpy as np
import ml_dtypes


def mxq(x, axis, fmt="e4m3"):
    dtype, down = {"e4m3": (ml_dtypes.float8_e4m3fn, 7), "e5m2": (ml_dtypes.float8_e5m2, 14)}[fmt]
    v = np.moveaxis(np.asarray(x, np.float32).astype(ml_dtypes.bfloat16).astype(np.float64), axis, -1)
    blocks = v.reshape(v.shape[:-1] + (-1, 32))
    amax = np.abs(blocks).max(-1, keepdims=True)
    byte = np.maximum(np.where(amax > 0, np.frexp(amax)[1] - 1 + 127, 0) - down, 1)
    scale = np.exp2(byte - 127.0)
    codes = (blocks / scale).astype(np.float32).astype(dtype).astype(np.float64)
    return np.moveaxis((codes * scale).reshape(v.shape), -1, axis)


WIDE = False


def mx_kscale(k):
    if not WIDE:
        return np.ones(k)
    levels = np.array([10, -10, 5, -5, 0])
    if k % 512:
        return np.exp2(np.random.permutation(np.resize(levels, k // 32))).repeat(32)
    a = np.empty((k // 512, 16))
    for p in range(k // 512):
        a[p, :8] = np.random.permutation(np.resize(levels, 8))
        for g in range(8):
            far = levels[np.abs(levels - a[p, g]) >= 10]
            a[p, g + 8] = far[np.random.randint(len(far))]
    return np.exp2(a.ravel()).repeat(32)


def f64(x):
    return np.asarray(x).astype(np.float64)


def striped8(idx):
    return np.asarray(idx).reshape(8, -1, 16).transpose(0, 2, 1).reshape(128, -1).astype(np.uint16)


def unstriped8(offs):
    return offs.reshape(8, 16, -1).transpose(0, 2, 1).reshape(8, -1).astype(np.int64)


def pick8(x, idx, run):
    r = np.arange(len(x))
    return x[r[:, None], idx[r % (8 * run) // run]]


E2M1 = np.array([0.0, 0.5, 1.0, 1.5, 2.0, 3.0, 4.0, 6.0, -0.0, -0.5, -1.0, -1.5, -2.0, -3.0, -4.0, -6.0])


def pack_weight(w, fmt):
    k, n = w.shape
    w = f64(np.asarray(w, np.float32).astype(ml_dtypes.bfloat16)).reshape(k // 32, 32, n)
    amax = np.abs(w).max(1)
    if fmt == "e4m3":
        byte = np.frexp(amax)[1] - 1 + 127 - 7
    else:
        mant, ex = np.frexp(amax / 6.0)
        byte = np.where(mant > 0.5, ex, ex - 1) + 127
    byte = np.clip(np.where(amax > 0, byte, 1), 1, 254)
    scaled = (w * np.exp2(127.0 - byte)[:, None, :]).reshape(k, n).astype(np.float32)
    by_word = np.ascontiguousarray(scaled.reshape(k // 512, 128, 4, n).transpose(0, 1, 3, 2))
    if fmt == "e4m3":
        words = by_word.astype(ml_dtypes.float8_e4m3fn).view(np.uint8)
    else:
        c = by_word.astype(ml_dtypes.float4_e2m1fn).view(np.uint8) & 0xF
        words = (c[..., 0::2] | (c[..., 1::2] << 4)).reshape(k // 512, 128, 2 * n)
    return np.ascontiguousarray(words), np.ascontiguousarray(byte.astype(np.uint8).reshape(k // 512, 16, n))


def unpack_weight(words, scales, fmt):
    g, _, n = scales.shape
    words = np.ascontiguousarray(words).reshape(g, 128, n, -1)
    if fmt == "e4m3":
        vals = words.view(ml_dtypes.float8_e4m3fn).astype(np.float64)
    else:
        nib = np.empty((g, 128, n, 4), np.uint8)
        nib[..., 0::2] = words & 0xF
        nib[..., 1::2] = words >> 4
        vals = E2M1[nib]
    vals = vals * np.repeat(np.exp2(scales.astype(np.float64) - 127.0), 8, axis=1)[..., None]
    return vals.transpose(0, 1, 3, 2).reshape(g * 512, n)


def sigmoid(v):
    return 1.0 / (1.0 + np.exp(-v))


D, T, I, Q = 512, 1024, 512, 128


def setup_inputs():
    n = np.random.standard_normal
    idx = np.stack([np.random.permutation(T)[:I] for _ in range(8)])
    idx2 = np.stack([np.random.permutation(T)[:I] for _ in range(8)])
    idx3 = np.stack([np.random.permutation(T)[:I] for _ in range(8)])
    idx4 = np.stack([np.random.permutation(T)[:I] for _ in range(8)])
    fd = mx_kscale(D)
    keysp = pack_weight(n((D, T)) / fd[:, None], "e4m3")
    return {
        "query": (n((D, Q)) * 1.2 / np.sqrt(D) * fd[:, None]).astype(np.float32),
        "keys_words": keysp[0],
        "keys_scales": keysp[1],
        "lam": (np.random.uniform(0.5, 1.5, (Q, 1))).astype(np.float32),
        "averse": (np.random.uniform(0.4, 1.0, (Q, 1))).astype(np.float32),
        "old": (np.random.uniform(0.0, 2.0, (Q, T))).astype(np.float32),
        "gainm": (np.random.uniform(0.5, 1.5, (Q, I))).astype(np.float32),
        "offs": striped8(idx),
        "offs2": striped8(idx2),
        "offs3": striped8(idx3),
        "offs4": striped8(idx4),
    }


def reference(query, keys_words, keys_scales, lam, averse, old, gainm, offs, offs2, offs3, offs4):
    idx = unstriped8(offs)
    idx2 = unstriped8(offs2)
    idx3 = unstriped8(offs3)
    idx4 = unstriped8(offs4)
    keysu = unpack_weight(keys_words, keys_scales, "e4m3")
    queryq = mxq(f64(query), 0, "e4m3")
    a = queryq.T @ keysu
    g1 = sigmoid(pick8(a, idx2, 16) * 2.0)
    s = (pick8(a, idx, 16) * g1 + pick8(a, idx3, 16) * (1.0 - g1)) * f64(lam)
    p = np.exp(s - np.max(s, axis=1, keepdims=True))
    r = p / np.sum(p, axis=1, keepdims=True)
    p2 = np.exp(s * (-1.0) - np.max(s * (-1.0), axis=1, keepdims=True))
    r2 = p2 / np.sum(p2, axis=1, keepdims=True)
    w = r - r2 * f64(averse)
    ws = w * f64(gainm) * 256.0
    wf = np.zeros((Q, T))
    wf[np.arange(Q)[:, None], idx4[np.arange(Q) % 128 // 16]] = ws
    y = f64(old) + wf
    return y

@@ -1,0 +1,159 @@
+from contextlib import ExitStack
+
+import concourse.mybir as mybir
+
+D, T, SLOTS, Q = 512, 1024, 512, 128
+FLOPS = 2 * D * Q * T
+
+F32 = mybir.dt.float32
+BF16 = mybir.dt.bfloat16
+I32 = mybir.dt.int32
+U32 = mybir.dt.uint32
+U16 = mybir.dt.uint16
+U8 = mybir.dt.uint8
+FP8X4 = mybir.dt.float8_e4m3fn_x4
+ALU = mybir.AluOpType
+ACT = mybir.ActivationFunctionType
+
+P = 128
+PACK = 4
+KEY_LOAD = 512
+MM_N = 256
+HALF = SLOTS // 2
+LIST_COLS = SLOTS // 16
+STORE_COLS = 256
+
+
+def tile_attend_conditioned_twoside_moved_heads_kernel(
+    tc, query, keys_words, keys_scales, lam, averse, old, gainm, offs, offs2, offs3, offs4, out
+):
+    nc = tc.nc
+    with ExitStack() as ctx:
+        sb = ctx.enter_context(tc.tile_pool(name="sb", bufs=1))
+        ps = ctx.enter_context(tc.psum_pool(name="ps", bufs=1))
+
+        key_scales = sb.tile([P, T], U8, name="key_scales", align_bytes=64)
+        nc.vector.memset(key_scales[:].bitcast(U32), 0)
+
+        q_raw = sb.tile([P, PACK, Q], F32, name="q_raw")
+        nc.sync.dma_start(out=q_raw[:], in_=query.rearrange("(p j) q -> p j q", j=PACK))
+        words = keys_words[0].rearrange("p n t -> p (n t)")
+        key_words = []
+        for c in range(T // KEY_LOAD):
+            kw = sb.tile([P, KEY_LOAD], U32, name=f"key_words{c}", align_bytes=64)
+            nc.sync.dma_start(
+                out=kw[:].bitcast(I32),
+                in_=words[:, c * KEY_LOAD * PACK : (c + 1) * KEY_LOAD * PACK].bitcast(I32),
+            )
+            key_words.append(kw)
+        for quad in range(4):
+            nc.scalar.dma_start(
+                out=key_scales[32 * quad : 32 * quad + 4, :].bitcast(I32),
+                in_=keys_scales[0, 4 * quad : 4 * quad + 4, :].bitcast(I32),
+            )
+        second_list = sb.tile([P, LIST_COLS], U16, name="second_list")
+        nc.sync.dma_start(second_list[:], offs3)
+        judge_list = sb.tile([P, LIST_COLS], U16, name="judge_list")
+        nc.sync.dma_start(judge_list[:], offs2)
+        first_list = sb.tile([P, LIST_COLS], U16, name="first_list")
+        nc.sync.dma_start(first_list[:], offs)
+        lam_col = sb.tile([P, 1], F32, name="lam_col")
+        nc.sync.dma_start(out=lam_col[:], in_=lam)
+        gain = sb.tile([P, SLOTS], F32, name="gain")
+        nc.sync.dma_start(out=gain[:], in_=gainm)
+        averse_col = sb.tile([P, 1], F32, name="averse_col")
+        nc.sync.dma_start(out=averse_col[:], in_=averse)
+        place_list = sb.tile([P, LIST_COLS], U16, name="place_list")
+        nc.sync.dma_start(place_list[:], offs4)
+        result = sb.tile([P, T], F32, name="result")
+        nc.sync.dma_start(out=result[:], in_=old)
+
+        placed = sb.tile([P, T], F32, name="placed")
+        nc.vector.memset(placed[:], 0.0)
+
+        q_bf = sb.tile([P, Q, PACK], BF16, name="q_bf", align_bytes=64)
+        nc.vector.tensor_copy(out=q_bf[:], in_=q_raw[:].rearrange("p j q -> p q j"))
+        q_words = sb.tile([P, Q], U32, name="q_words", align_bytes=64)
+        q_scales = sb.tile([P, Q], U8, name="q_scales", align_bytes=64)
+        nc.vector.quantize_mx(
+            out=q_words[:].bitcast(FP8X4), scales=q_scales[:], in_=q_bf[:].rearrange("p q j -> p (q j)")
+        )
+
+        scores = sb.tile([P, T], F32, name="scores")
+        for c in range(T // MM_N):
+            bank = ps.tile([P, MM_N], F32, name=f"bank{c}")
+            load, at = divmod(c * MM_N, KEY_LOAD)
+            cols = slice(c * MM_N, (c + 1) * MM_N)
+            nc.tensor.matmul_mx(
+                out=bank[:],
+                lhsT=q_words[:].bitcast(FP8X4),
+                lhsT_scale=q_scales[:],
+                rhs=key_words[load][:, at : at + MM_N].bitcast(FP8X4),
+                rhs_scale=key_scales[:, cols],
+                start=True,
+                stop=True,
+            )
+            if c % 2 == 0:
+                nc.vector.tensor_copy(out=scores[:, cols], in_=bank[:])
+            else:
+                nc.scalar.copy(out=scores[:, cols], in_=bank[:])
+
+        def look_up(list_tile, h):
+            return scores[:].indirect(list_tile[:, h * LIST_COLS // 2 : (h + 1) * LIST_COLS // 2])
+
+        def half(tile, h):
+            return tile[:, h * HALF : (h + 1) * HALF]
+
+        second = sb.tile([P, SLOTS], F32, name="second")
+        judge = sb.tile([P, SLOTS], F32, name="judge", tag="judge_then_gain")
+        gate = sb.tile([P, SLOTS], F32, name="gate")
+        gap = sb.tile([P, SLOTS], F32, name="gap")
+        pull = sb.tile([P, SLOTS], F32, name="pull")
+        mixed = sb.tile([P, SLOTS], F32, name="mixed")
+        score = sb.tile([P, SLOTS], F32, name="score")
+
+        nc.vector.tensor_copy(half(second, 0), look_up(second_list, 0))
+        nc.scalar.activation(half(second, 1), look_up(second_list, 1), ACT.Copy)
+        for h in range(2):
+            nc.scalar.activation(half(judge, h), look_up(judge_list, h), ACT.Copy)
+            nc.scalar.activation(half(gate, h), half(judge, h), ACT.Tanh)
+        for h in range(2):
+            nc.vector.tensor_tensor(half(gap, h), look_up(first_list, h), half(second, h), ALU.subtract)
+        lowest = [sb.tile([P, 1], F32, name=f"lowest{h}") for h in range(2)]
+        for h in range(2):
+            nc.vector.scalar_tensor_tensor(half(pull, h), half(gate, h), 1.0, half(gap, h), ALU.add, ALU.mult)
+        for h in range(2):
+            nc.vector.scalar_tensor_tensor(half(mixed, h), half(pull, h), 0.5, half(second, h), ALU.mult, ALU.add)
+        for h in range(2):
+            nc.vector.tensor_scalar(
+                half(score, h), half(mixed, h), lam_col[:], lowest[0][:] if h else None,
+                ALU.mult, ALU.min, accum_out=lowest[h][:],
+            )
+        neg_highest = sb.tile([P, 1], F32, name="neg_highest")
+        nc.vector.tensor_reduce(neg_highest[:], score[:], mybir.AxisListType.X, ALU.max, negate=True)
+
+        gain256 = sb.tile([P, SLOTS], F32, name="gain256", tag="judge_then_gain")
+        nc.scalar.activation(gain256[:], gain[:], ACT.Copy, scale=256.0)
+
+        p_low = sb.tile([P, SLOTS], F32, name="p_low")
+        sum_low = sb.tile([P, 1], F32, name="sum_low")
+        nc.scalar.activation(p_low[:], score[:], ACT.Exp, bias=lowest[1][:], scale=-1.0, accum_out=sum_low[:])
+        p_high = sb.tile([P, SLOTS], F32, name="p_high")
+        sum_high = sb.tile([P, 1], F32, name="sum_high")
+        nc.scalar.activation(p_high[:], score[:], ACT.Exp, bias=neg_highest[:], accum_out=sum_high[:])
+
+        inv_low = sb.tile([P, 1], F32, name="inv_low")
+        nc.vector.reciprocal(inv_low[:], sum_low[:])
+        avoided = sb.tile([P, SLOTS], F32, name="avoided")
+        nc.vector.tensor_scalar(avoided[:], p_low[:], inv_low[:], averse_col[:], ALU.mult, ALU.mult)
+        inv_high = sb.tile([P, 1], F32, name="inv_high")
+        nc.vector.reciprocal(inv_high[:], sum_high[:])
+        weight = sb.tile([P, SLOTS], F32, name="weight")
+        nc.vector.scalar_tensor_tensor(weight[:], p_high[:], inv_high[:], avoided[:], ALU.mult, ALU.subtract)
+        nc.vector.tensor_tensor(placed[:].indirect(place_list[:]), weight[:], gain256[:], ALU.mult)
+
+        for c in range(T // STORE_COLS):
+            cols = slice(c * STORE_COLS, (c + 1) * STORE_COLS)
+            nc.vector.tensor_tensor(result[:, cols], placed[:, cols], result[:, cols], ALU.add)
+            queue = nc.sync if c % 2 == 0 else nc.scalar
+            queue.dma_start(out=out[:, cols], in_=result[:, cols])

@@ -37,6 +37,13 @@ def tile_attend_conditioned_twoside_moved_heads_kernel(
 
         q_raw = sb.tile([P, PACK, Q], F32, name="q_raw")
         nc.sync.dma_start(out=q_raw[:], in_=query.rearrange("(p j) q -> p j q", j=PACK))
+        judge_list = sb.tile([P, LIST_COLS], U16, name="judge_list")
+        nc.sync.dma_start(judge_list[:], offs2)
+        for quad in range(4):
+            nc.sync.dma_start(
+                out=key_scales[32 * quad : 32 * quad + 4, :].bitcast(I32),
+                in_=keys_scales[0, 4 * quad : 4 * quad + 4, :].bitcast(I32),
+            )
         words = keys_words[0].rearrange("p n t -> p (n t)")
         key_words = []
         for c in range(T // KEY_LOAD):
@@ -46,15 +53,8 @@ def tile_attend_conditioned_twoside_moved_heads_kernel(
                 in_=words[:, c * KEY_LOAD * PACK : (c + 1) * KEY_LOAD * PACK].bitcast(I32),
             )
             key_words.append(kw)
-        for quad in range(4):
-            nc.scalar.dma_start(
-                out=key_scales[32 * quad : 32 * quad + 4, :].bitcast(I32),
-                in_=keys_scales[0, 4 * quad : 4 * quad + 4, :].bitcast(I32),
-            )
         second_list = sb.tile([P, LIST_COLS], U16, name="second_list")
         nc.sync.dma_start(second_list[:], offs3)
-        judge_list = sb.tile([P, LIST_COLS], U16, name="judge_list")
-        nc.sync.dma_start(judge_list[:], offs2)
         first_list = sb.tile([P, LIST_COLS], U16, name="first_list")
         nc.sync.dma_start(first_list[:], offs)
         lam_col = sb.tile([P, 1], F32, name="lam_col")
@@ -93,10 +93,7 @@ def tile_attend_conditioned_twoside_moved_heads_kernel(
                 start=True,
                 stop=True,
             )
-            if c % 2 == 0:
-                nc.vector.tensor_copy(out=scores[:, cols], in_=bank[:])
-            else:
-                nc.scalar.copy(out=scores[:, cols], in_=bank[:])
+            nc.vector.tensor_copy(out=scores[:, cols], in_=bank[:])
 
         def look_up(list_tile, h):
             return scores[:].indirect(list_tile[:, h * LIST_COLS // 2 : (h + 1) * LIST_COLS // 2])
@@ -105,42 +102,42 @@ def tile_attend_conditioned_twoside_moved_heads_kernel(
             return tile[:, h * HALF : (h + 1) * HALF]
 
         second = sb.tile([P, SLOTS], F32, name="second")
-        judge = sb.tile([P, SLOTS], F32, name="judge", tag="judge_then_gain")
         gate = sb.tile([P, SLOTS], F32, name="gate")
         gap = sb.tile([P, SLOTS], F32, name="gap")
         pull = sb.tile([P, SLOTS], F32, name="pull")
         mixed = sb.tile([P, SLOTS], F32, name="mixed")
+
+        neg_lam = sb.tile([P, 1], F32, name="neg_lam")
+        nc.gpsimd.tensor_scalar(neg_lam[:], lam_col[:], -1.0, 0.0, ALU.mult, ALU.add)
+
+        nc.scalar.activation(half(gate, 1), look_up(judge_list, 1), ACT.Sigmoid, scale=2.0)
+        nc.vector.tensor_copy(half(second, 1), look_up(second_list, 1))
+        nc.scalar.activation(half(second, 0), look_up(second_list, 0), ACT.Copy)
+        nc.scalar.activation(half(gate, 0), look_up(judge_list, 0), ACT.Sigmoid, scale=2.0)
+        first = sb.tile([P, HALF], F32, name="first")
+        nc.vector.tensor_copy(first[:], look_up(first_list, 0))
+        nc.vector.tensor_tensor(half(gap, 1), look_up(first_list, 1), half(second, 1), ALU.subtract)
+        nc.vector.tensor_tensor(half(gap, 0), first[:], half(second, 0), ALU.subtract)
+        for h in (1, 0):
+            nc.vector.tensor_tensor(half(pull, h), half(gate, h), half(gap, h), ALU.mult)
+        for h in (1, 0):
+            nc.vector.tensor_tensor(half(mixed, h), half(pull, h), half(second, h), ALU.add)
         score = sb.tile([P, SLOTS], F32, name="score")
-
-        nc.vector.tensor_copy(half(second, 0), look_up(second_list, 0))
-        nc.scalar.activation(half(second, 1), look_up(second_list, 1), ACT.Copy)
-        for h in range(2):
-            nc.scalar.activation(half(judge, h), look_up(judge_list, h), ACT.Copy)
-            nc.scalar.activation(half(gate, h), half(judge, h), ACT.Tanh)
-        for h in range(2):
-            nc.vector.tensor_tensor(half(gap, h), look_up(first_list, h), half(second, h), ALU.subtract)
-        lowest = [sb.tile([P, 1], F32, name=f"lowest{h}") for h in range(2)]
-        for h in range(2):
-            nc.vector.scalar_tensor_tensor(half(pull, h), half(gate, h), 1.0, half(gap, h), ALU.add, ALU.mult)
-        for h in range(2):
-            nc.vector.scalar_tensor_tensor(half(mixed, h), half(pull, h), 0.5, half(second, h), ALU.mult, ALU.add)
-        for h in range(2):
-            nc.vector.tensor_scalar(
-                half(score, h), half(mixed, h), lam_col[:], lowest[0][:] if h else None,
-                ALU.mult, ALU.min, accum_out=lowest[h][:],
-            )
+        lowest = sb.tile([P, 1], F32, name="lowest")
+        nc.vector.tensor_scalar(score[:], mixed[:], lam_col[:], None, ALU.mult, ALU.min, accum_out=lowest[:])
+        neg_score = sb.tile([P, SLOTS], F32, name="neg_score", tag="neg_score_then_gain")
         neg_highest = sb.tile([P, 1], F32, name="neg_highest")
-        nc.vector.tensor_reduce(neg_highest[:], score[:], mybir.AxisListType.X, ALU.max, negate=True)
-
-        gain256 = sb.tile([P, SLOTS], F32, name="gain256", tag="judge_then_gain")
-        nc.scalar.activation(gain256[:], gain[:], ACT.Copy, scale=256.0)
+        nc.vector.tensor_scalar(neg_score[:], mixed[:], neg_lam[:], None, ALU.mult, ALU.min, accum_out=neg_highest[:])
 
         p_low = sb.tile([P, SLOTS], F32, name="p_low")
         sum_low = sb.tile([P, 1], F32, name="sum_low")
-        nc.scalar.activation(p_low[:], score[:], ACT.Exp, bias=lowest[1][:], scale=-1.0, accum_out=sum_low[:])
+        nc.scalar.activation(p_low[:], score[:], ACT.Exp, bias=lowest[:], scale=-1.0, accum_out=sum_low[:])
         p_high = sb.tile([P, SLOTS], F32, name="p_high")
         sum_high = sb.tile([P, 1], F32, name="sum_high")
-        nc.scalar.activation(p_high[:], score[:], ACT.Exp, bias=neg_highest[:], accum_out=sum_high[:])
+        nc.scalar.activation(p_high[:], neg_score[:], ACT.Exp, bias=neg_highest[:], scale=-1.0, accum_out=sum_high[:])
+
+        gain256 = sb.tile([P, SLOTS], F32, name="gain256", tag="neg_score_then_gain")
+        nc.scalar.activation(gain256[:], gain[:], ACT.Copy, scale=256.0)
 
         inv_low = sb.tile([P, 1], F32, name="inv_low")
         nc.vector.reciprocal(inv_low[:], sum_low[:])

@@ -18,7 +18,7 @@ ACT = mybir.ActivationFunctionType
 P = 128
 PACK = 4
 KEY_LOAD = 512
-MM_N = 256
+MM_WIDTHS = (256, 256, 256, 128, 128)
 HALF = SLOTS // 2
 LIST_COLS = SLOTS // 16
 STORE_COLS = 256
@@ -37,8 +37,8 @@ def tile_attend_conditioned_twoside_moved_heads_kernel(
 
         q_raw = sb.tile([P, PACK, Q], F32, name="q_raw")
         nc.sync.dma_start(out=q_raw[:], in_=query.rearrange("(p j) q -> p j q", j=PACK))
-        judge_list = sb.tile([P, LIST_COLS], U16, name="judge_list")
-        nc.sync.dma_start(judge_list[:], offs2)
+        second_list = sb.tile([P, LIST_COLS], U16, name="second_list")
+        nc.sync.dma_start(second_list[:], offs3)
         for quad in range(4):
             nc.sync.dma_start(
                 out=key_scales[32 * quad : 32 * quad + 4, :].bitcast(I32),
@@ -53,8 +53,8 @@ def tile_attend_conditioned_twoside_moved_heads_kernel(
                 in_=words[:, c * KEY_LOAD * PACK : (c + 1) * KEY_LOAD * PACK].bitcast(I32),
             )
             key_words.append(kw)
-        second_list = sb.tile([P, LIST_COLS], U16, name="second_list")
-        nc.sync.dma_start(second_list[:], offs3)
+        judge_list = sb.tile([P, LIST_COLS], U16, name="judge_list")
+        nc.sync.dma_start(judge_list[:], offs2)
         first_list = sb.tile([P, LIST_COLS], U16, name="first_list")
         nc.sync.dma_start(first_list[:], offs)
         lam_col = sb.tile([P, 1], F32, name="lam_col")
@@ -71,29 +71,41 @@ def tile_attend_conditioned_twoside_moved_heads_kernel(
         placed = sb.tile([P, T], F32, name="placed")
         nc.vector.memset(placed[:], 0.0)
 
-        q_bf = sb.tile([P, Q, PACK], BF16, name="q_bf", align_bytes=64)
-        nc.vector.tensor_copy(out=q_bf[:], in_=q_raw[:].rearrange("p j q -> p q j"))
+        warm = sb.tile([P, 1], F32, name="warm")
+        nc.gpsimd.memset(warm[:], 0.0)
+        nc.scalar.activation(warm[:], warm[:], ACT.Sigmoid)
+
         q_words = sb.tile([P, Q], U32, name="q_words", align_bytes=64)
         q_scales = sb.tile([P, Q], U8, name="q_scales", align_bytes=64)
-        nc.vector.quantize_mx(
-            out=q_words[:].bitcast(FP8X4), scales=q_scales[:], in_=q_bf[:].rearrange("p q j -> p (q j)")
-        )
+        q_bf = [sb.tile([P, Q // 2, PACK], BF16, name=f"q_bf{h}", align_bytes=64) for h in range(2)]
+        nc.vector.tensor_copy(out=q_bf[0][:], in_=q_raw[:, :, : Q // 2].rearrange("p j q -> p q j"))
+        nc.vector.tensor_copy(out=q_bf[1][:], in_=q_raw[:, :, Q // 2 :].rearrange("p j q -> p q j"))
+        for h in range(2):
+            cols = slice(h * Q // 2, (h + 1) * Q // 2)
+            nc.vector.quantize_mx(
+                out=q_words[:, cols].bitcast(FP8X4), scales=q_scales[:, cols], in_=q_bf[h][:].rearrange("p q j -> p (q j)")
+            )
 
         scores = sb.tile([P, T], F32, name="scores")
-        for c in range(T // MM_N):
-            bank = ps.tile([P, MM_N], F32, name=f"bank{c}")
-            load, at = divmod(c * MM_N, KEY_LOAD)
-            cols = slice(c * MM_N, (c + 1) * MM_N)
+        start = 0
+        for c, width in enumerate(MM_WIDTHS):
+            bank = ps.tile([P, width], F32, name=f"bank{c}")
+            load, at = divmod(start, KEY_LOAD)
+            cols = slice(start, start + width)
+            start = start + width
             nc.tensor.matmul_mx(
                 out=bank[:],
                 lhsT=q_words[:].bitcast(FP8X4),
                 lhsT_scale=q_scales[:],
-                rhs=key_words[load][:, at : at + MM_N].bitcast(FP8X4),
+                rhs=key_words[load][:, at : at + width].bitcast(FP8X4),
                 rhs_scale=key_scales[:, cols],
                 start=True,
                 stop=True,
             )
-            nc.vector.tensor_copy(out=scores[:, cols], in_=bank[:])
+            if c % 2 == 0:
+                nc.vector.tensor_copy(out=scores[:, cols], in_=bank[:])
+            else:
+                nc.scalar.copy(out=scores[:, cols], in_=bank[:])
 
         def look_up(list_tile, h):
             return scores[:].indirect(list_tile[:, h * LIST_COLS // 2 : (h + 1) * LIST_COLS // 2])
@@ -105,38 +117,31 @@ def tile_attend_conditioned_twoside_moved_heads_kernel(
         gate = sb.tile([P, SLOTS], F32, name="gate")
         gap = sb.tile([P, SLOTS], F32, name="gap")
         pull = sb.tile([P, SLOTS], F32, name="pull")
-        mixed = sb.tile([P, SLOTS], F32, name="mixed")
+        score = sb.tile([P, SLOTS], F32, name="score", tag="score_then_gain")
 
-        neg_lam = sb.tile([P, 1], F32, name="neg_lam")
-        nc.gpsimd.tensor_scalar(neg_lam[:], lam_col[:], -1.0, 0.0, ALU.mult, ALU.add)
-
-        nc.scalar.activation(half(gate, 1), look_up(judge_list, 1), ACT.Sigmoid, scale=2.0)
-        nc.vector.tensor_copy(half(second, 1), look_up(second_list, 1))
         nc.scalar.activation(half(second, 0), look_up(second_list, 0), ACT.Copy)
-        nc.scalar.activation(half(gate, 0), look_up(judge_list, 0), ACT.Sigmoid, scale=2.0)
-        first = sb.tile([P, HALF], F32, name="first")
-        nc.vector.tensor_copy(first[:], look_up(first_list, 0))
-        nc.vector.tensor_tensor(half(gap, 1), look_up(first_list, 1), half(second, 1), ALU.subtract)
-        nc.vector.tensor_tensor(half(gap, 0), first[:], half(second, 0), ALU.subtract)
-        for h in (1, 0):
-            nc.vector.tensor_tensor(half(pull, h), half(gate, h), half(gap, h), ALU.mult)
-        for h in (1, 0):
-            nc.vector.tensor_tensor(half(mixed, h), half(pull, h), half(second, h), ALU.add)
-        score = sb.tile([P, SLOTS], F32, name="score")
+        nc.vector.tensor_copy(half(second, 1), look_up(second_list, 1))
+        for h in range(2):
+            nc.scalar.activation(half(gate, h), look_up(judge_list, h), ACT.Sigmoid, scale=2.0)
+        for h in range(2):
+            nc.vector.tensor_tensor(half(gap, h), look_up(first_list, h), half(second, h), ALU.subtract)
+        for h in range(2):
+            nc.vector.scalar_tensor_tensor(half(pull, h), half(gate, h), lam_col[:], half(gap, h), ALU.mult, ALU.mult)
+        for h in range(2):
+            nc.vector.scalar_tensor_tensor(half(score, h), half(second, h), lam_col[:], half(pull, h), ALU.mult, ALU.add)
         lowest = sb.tile([P, 1], F32, name="lowest")
-        nc.vector.tensor_scalar(score[:], mixed[:], lam_col[:], None, ALU.mult, ALU.min, accum_out=lowest[:])
-        neg_score = sb.tile([P, SLOTS], F32, name="neg_score", tag="neg_score_then_gain")
+        nc.vector.tensor_reduce(lowest[:], score[:], mybir.AxisListType.X, ALU.min)
         neg_highest = sb.tile([P, 1], F32, name="neg_highest")
-        nc.vector.tensor_scalar(neg_score[:], mixed[:], neg_lam[:], None, ALU.mult, ALU.min, accum_out=neg_highest[:])
+        nc.vector.tensor_reduce(neg_highest[:], score[:], mybir.AxisListType.X, ALU.max, negate=True)
 
         p_low = sb.tile([P, SLOTS], F32, name="p_low")
         sum_low = sb.tile([P, 1], F32, name="sum_low")
         nc.scalar.activation(p_low[:], score[:], ACT.Exp, bias=lowest[:], scale=-1.0, accum_out=sum_low[:])
         p_high = sb.tile([P, SLOTS], F32, name="p_high")
         sum_high = sb.tile([P, 1], F32, name="sum_high")
-        nc.scalar.activation(p_high[:], neg_score[:], ACT.Exp, bias=neg_highest[:], scale=-1.0, accum_out=sum_high[:])
+        nc.scalar.activation(p_high[:], score[:], ACT.Exp, bias=neg_highest[:], accum_out=sum_high[:])
 
-        gain256 = sb.tile([P, SLOTS], F32, name="gain256", tag="neg_score_then_gain")
+        gain256 = sb.tile([P, SLOTS], F32, name="gain256", tag="score_then_gain")
         nc.scalar.activation(gain256[:], gain[:], ACT.Copy, scale=256.0)
 
         inv_low = sb.tile([P, 1], F32, name="inv_low")

@@ -71,10 +71,6 @@ def tile_attend_conditioned_twoside_moved_heads_kernel(
         placed = sb.tile([P, T], F32, name="placed")
         nc.vector.memset(placed[:], 0.0)
 
-        warm = sb.tile([P, 1], F32, name="warm")
-        nc.gpsimd.memset(warm[:], 0.0)
-        nc.scalar.activation(warm[:], warm[:], ACT.Sigmoid)
-
         q_words = sb.tile([P, Q], U32, name="q_words", align_bytes=64)
         q_scales = sb.tile([P, Q], U8, name="q_scales", align_bytes=64)
         q_bf = [sb.tile([P, Q // 2, PACK], BF16, name=f"q_bf{h}", align_bytes=64) for h in range(2)]

@@ -17,6 +17,8 @@ ACT = mybir.ActivationFunctionType
 
 P = 128
 PACK = 4
+QUADRANT = 32
+SCALE_ROWS = 4
 KEY_LOAD = 512
 MM_WIDTHS = (256, 256, 256, 128, 128)
 HALF = SLOTS // 2
@@ -39,20 +41,20 @@ def tile_attend_conditioned_twoside_moved_heads_kernel(
         nc.sync.dma_start(out=q_raw[:], in_=query.rearrange("(p j) q -> p j q", j=PACK))
         second_list = sb.tile([P, LIST_COLS], U16, name="second_list")
         nc.sync.dma_start(second_list[:], offs3)
-        for quad in range(4):
+        for quad in range(P // QUADRANT):
             nc.sync.dma_start(
-                out=key_scales[32 * quad : 32 * quad + 4, :].bitcast(I32),
-                in_=keys_scales[0, 4 * quad : 4 * quad + 4, :].bitcast(I32),
+                out=key_scales[QUADRANT * quad : QUADRANT * quad + SCALE_ROWS, :].bitcast(I32),
+                in_=keys_scales[0, SCALE_ROWS * quad : SCALE_ROWS * (quad + 1), :].bitcast(I32),
             )
-        words = keys_words[0].rearrange("p n t -> p (n t)")
+        key_bytes = keys_words[0].rearrange("p n t -> p (n t)")
         key_words = []
         for c in range(T // KEY_LOAD):
-            kw = sb.tile([P, KEY_LOAD], U32, name=f"key_words{c}", align_bytes=64)
+            loaded = sb.tile([P, KEY_LOAD], U32, name=f"key_words{c}", align_bytes=64)
             nc.sync.dma_start(
-                out=kw[:].bitcast(I32),
-                in_=words[:, c * KEY_LOAD * PACK : (c + 1) * KEY_LOAD * PACK].bitcast(I32),
+                out=loaded[:].bitcast(I32),
+                in_=key_bytes[:, c * KEY_LOAD * PACK : (c + 1) * KEY_LOAD * PACK].bitcast(I32),
             )
-            key_words.append(kw)
+            key_words.append(loaded)
         judge_list = sb.tile([P, LIST_COLS], U16, name="judge_list")
         nc.sync.dma_start(judge_list[:], offs2)
         first_list = sb.tile([P, LIST_COLS], U16, name="first_list")
@@ -71,18 +73,23 @@ def tile_attend_conditioned_twoside_moved_heads_kernel(
         placed = sb.tile([P, T], F32, name="placed")
         nc.vector.memset(placed[:], 0.0)
 
+        warm = sb.tile([P, 1], F32, name="warm")
+        nc.scalar.activation(warm[:], q_raw[:, 0, 0:1], ACT.Sigmoid)
+
         q_words = sb.tile([P, Q], U32, name="q_words", align_bytes=64)
         q_scales = sb.tile([P, Q], U8, name="q_scales", align_bytes=64)
+        q_halves = [slice(0, Q // 2), slice(Q // 2, Q)]
         q_bf = [sb.tile([P, Q // 2, PACK], BF16, name=f"q_bf{h}", align_bytes=64) for h in range(2)]
-        nc.vector.tensor_copy(out=q_bf[0][:], in_=q_raw[:, :, : Q // 2].rearrange("p j q -> p q j"))
-        nc.vector.tensor_copy(out=q_bf[1][:], in_=q_raw[:, :, Q // 2 :].rearrange("p j q -> p q j"))
-        for h in range(2):
-            cols = slice(h * Q // 2, (h + 1) * Q // 2)
+        for h, rows in enumerate(q_halves):
+            nc.vector.tensor_copy(out=q_bf[h][:], in_=q_raw[:, :, rows].rearrange("p j q -> p q j"))
+        for h, rows in enumerate(q_halves):
             nc.vector.quantize_mx(
-                out=q_words[:, cols].bitcast(FP8X4), scales=q_scales[:, cols], in_=q_bf[h][:].rearrange("p q j -> p (q j)")
+                out=q_words[:, rows].bitcast(FP8X4),
+                scales=q_scales[:, rows],
+                in_=q_bf[h][:].rearrange("p q j -> p (q j)"),
             )
 
-        scores = sb.tile([P, T], F32, name="scores")
+        products = sb.tile([P, T], F32, name="scores")
         start = 0
         for c, width in enumerate(MM_WIDTHS):
             bank = ps.tile([P, width], F32, name=f"bank{c}")
@@ -99,12 +106,12 @@ def tile_attend_conditioned_twoside_moved_heads_kernel(
                 stop=True,
             )
             if c % 2 == 0:
-                nc.vector.tensor_copy(out=scores[:, cols], in_=bank[:])
+                nc.vector.tensor_copy(out=products[:, cols], in_=bank[:])
             else:
-                nc.scalar.copy(out=scores[:, cols], in_=bank[:])
+                nc.scalar.copy(out=products[:, cols], in_=bank[:])
 
         def look_up(list_tile, h):
-            return scores[:].indirect(list_tile[:, h * LIST_COLS // 2 : (h + 1) * LIST_COLS // 2])
+            return products[:].indirect(list_tile[:, h * LIST_COLS // 2 : (h + 1) * LIST_COLS // 2])
 
         def half(tile, h):
             return tile[:, h * HALF : (h + 1) * HALF]
@@ -125,6 +132,7 @@ def tile_attend_conditioned_twoside_moved_heads_kernel(
             nc.vector.scalar_tensor_tensor(half(pull, h), half(gate, h), lam_col[:], half(gap, h), ALU.mult, ALU.mult)
         for h in range(2):
             nc.vector.scalar_tensor_tensor(half(score, h), half(second, h), lam_col[:], half(pull, h), ALU.mult, ALU.add)
+
         lowest = sb.tile([P, 1], F32, name="lowest")
         nc.vector.tensor_reduce(lowest[:], score[:], mybir.AxisListType.X, ALU.min)
         neg_highest = sb.tile([P, 1], F32, name="neg_highest")
@@ -148,6 +156,7 @@ def tile_attend_conditioned_twoside_moved_heads_kernel(
         nc.vector.reciprocal(inv_high[:], sum_high[:])
         weight = sb.tile([P, SLOTS], F32, name="weight")
         nc.vector.scalar_tensor_tensor(weight[:], p_high[:], inv_high[:], avoided[:], ALU.mult, ALU.subtract)
+
         nc.vector.tensor_tensor(placed[:].indirect(place_list[:]), weight[:], gain256[:], ALU.mult)
 
         for c in range(T // STORE_COLS):

from contextlib import ExitStack

import concourse.mybir as mybir

D, T, SLOTS, Q = 512, 1024, 512, 128
FLOPS = 2 * D * Q * T

F32 = mybir.dt.float32
BF16 = mybir.dt.bfloat16
I32 = mybir.dt.int32
U32 = mybir.dt.uint32
U16 = mybir.dt.uint16
U8 = mybir.dt.uint8
FP8X4 = mybir.dt.float8_e4m3fn_x4
ALU = mybir.AluOpType
ACT = mybir.ActivationFunctionType

P = 128
PACK = 4
QUADRANT = 32
SCALE_ROWS = 4
KEY_LOAD = 512
MM_WIDTHS = (256, 256, 256, 128, 128)
HALF = SLOTS // 2
LIST_COLS = SLOTS // 16
STORE_COLS = 256


def tile_attend_conditioned_twoside_moved_heads_kernel(
    tc, query, keys_words, keys_scales, lam, averse, old, gainm, offs, offs2, offs3, offs4, out
):
    nc = tc.nc
    with ExitStack() as ctx:
        sb = ctx.enter_context(tc.tile_pool(name="sb", bufs=1))
        ps = ctx.enter_context(tc.psum_pool(name="ps", bufs=1))

        key_scales = sb.tile([P, T], U8, name="key_scales", align_bytes=64)
        nc.vector.memset(key_scales[:].bitcast(U32), 0)

        q_raw = sb.tile([P, PACK, Q], F32, name="q_raw")
        nc.sync.dma_start(out=q_raw[:], in_=query.rearrange("(p j) q -> p j q", j=PACK))
        second_list = sb.tile([P, LIST_COLS], U16, name="second_list")
        nc.sync.dma_start(second_list[:], offs3)
        for quad in range(P // QUADRANT):
            nc.sync.dma_start(
                out=key_scales[QUADRANT * quad : QUADRANT * quad + SCALE_ROWS, :].bitcast(I32),
                in_=keys_scales[0, SCALE_ROWS * quad : SCALE_ROWS * (quad + 1), :].bitcast(I32),
            )
        key_bytes = keys_words[0].rearrange("p n t -> p (n t)")
        key_words = []
        for c in range(T // KEY_LOAD):
            loaded = sb.tile([P, KEY_LOAD], U32, name=f"key_words{c}", align_bytes=64)
            nc.sync.dma_start(
                out=loaded[:].bitcast(I32),
                in_=key_bytes[:, c * KEY_LOAD * PACK : (c + 1) * KEY_LOAD * PACK].bitcast(I32),
            )
            key_words.append(loaded)
        judge_list = sb.tile([P, LIST_COLS], U16, name="judge_list")
        nc.sync.dma_start(judge_list[:], offs2)
        first_list = sb.tile([P, LIST_COLS], U16, name="first_list")
        nc.sync.dma_start(first_list[:], offs)
        lam_col = sb.tile([P, 1], F32, name="lam_col")
        nc.sync.dma_start(out=lam_col[:], in_=lam)
        gain = sb.tile([P, SLOTS], F32, name="gain")
        nc.sync.dma_start(out=gain[:], in_=gainm)
        averse_col = sb.tile([P, 1], F32, name="averse_col")
        nc.sync.dma_start(out=averse_col[:], in_=averse)
        place_list = sb.tile([P, LIST_COLS], U16, name="place_list")
        nc.sync.dma_start(place_list[:], offs4)
        result = sb.tile([P, T], F32, name="result")
        nc.sync.dma_start(out=result[:], in_=old)

        placed = sb.tile([P, T], F32, name="placed")
        nc.vector.memset(placed[:], 0.0)

        warm = sb.tile([P, 1], F32, name="warm")
        nc.scalar.activation(warm[:], q_raw[:, 0, 0:1], ACT.Sigmoid)

        q_words = sb.tile([P, Q], U32, name="q_words", align_bytes=64)
        q_scales = sb.tile([P, Q], U8, name="q_scales", align_bytes=64)
        q_halves = [slice(0, Q // 2), slice(Q // 2, Q)]
        q_bf = [sb.tile([P, Q // 2, PACK], BF16, name=f"q_bf{h}", align_bytes=64) for h in range(2)]
        for h, rows in enumerate(q_halves):
            nc.vector.tensor_copy(out=q_bf[h][:], in_=q_raw[:, :, rows].rearrange("p j q -> p q j"))
        for h, rows in enumerate(q_halves):
            nc.vector.quantize_mx(
                out=q_words[:, rows].bitcast(FP8X4),
                scales=q_scales[:, rows],
                in_=q_bf[h][:].rearrange("p q j -> p (q j)"),
            )

        products = sb.tile([P, T], F32, name="scores")
        start = 0
        for c, width in enumerate(MM_WIDTHS):
            bank = ps.tile([P, width], F32, name=f"bank{c}")
            load, at = divmod(start, KEY_LOAD)
            cols = slice(start, start + width)
            start = start + width
            nc.tensor.matmul_mx(
                out=bank[:],
                lhsT=q_words[:].bitcast(FP8X4),
                lhsT_scale=q_scales[:],
                rhs=key_words[load][:, at : at + width].bitcast(FP8X4),
                rhs_scale=key_scales[:, cols],
                start=True,
                stop=True,
            )
            if c % 2 == 0:
                nc.vector.tensor_copy(out=products[:, cols], in_=bank[:])
            else:
                nc.scalar.copy(out=products[:, cols], in_=bank[:])

        def look_up(list_tile, h):
            return products[:].indirect(list_tile[:, h * LIST_COLS // 2 : (h + 1) * LIST_COLS // 2])

        def half(tile, h):
            return tile[:, h * HALF : (h + 1) * HALF]

        second = sb.tile([P, SLOTS], F32, name="second")
        gate = sb.tile([P, SLOTS], F32, name="gate")
        gap = sb.tile([P, SLOTS], F32, name="gap")
        pull = sb.tile([P, SLOTS], F32, name="pull")
        score = sb.tile([P, SLOTS], F32, name="score", tag="score_then_gain")

        nc.scalar.activation(half(second, 0), look_up(second_list, 0), ACT.Copy)
        nc.vector.tensor_copy(half(second, 1), look_up(second_list, 1))
        for h in range(2):
            nc.scalar.activation(half(gate, h), look_up(judge_list, h), ACT.Sigmoid, scale=2.0)
        for h in range(2):
            nc.vector.tensor_tensor(half(gap, h), look_up(first_list, h), half(second, h), ALU.subtract)
        for h in range(2):
            nc.vector.scalar_tensor_tensor(half(pull, h), half(gate, h), lam_col[:], half(gap, h), ALU.mult, ALU.mult)
        for h in range(2):
            nc.vector.scalar_tensor_tensor(half(score, h), half(second, h), lam_col[:], half(pull, h), ALU.mult, ALU.add)

        lowest = sb.tile([P, 1], F32, name="lowest")
        nc.vector.tensor_reduce(lowest[:], score[:], mybir.AxisListType.X, ALU.min)
        neg_highest = sb.tile([P, 1], F32, name="neg_highest")
        nc.vector.tensor_reduce(neg_highest[:], score[:], mybir.AxisListType.X, ALU.max, negate=True)

        p_low = sb.tile([P, SLOTS], F32, name="p_low")
        sum_low = sb.tile([P, 1], F32, name="sum_low")
        nc.scalar.activation(p_low[:], score[:], ACT.Exp, bias=lowest[:], scale=-1.0, accum_out=sum_low[:])
        p_high = sb.tile([P, SLOTS], F32, name="p_high")
        sum_high = sb.tile([P, 1], F32, name="sum_high")
        nc.scalar.activation(p_high[:], score[:], ACT.Exp, bias=neg_highest[:], accum_out=sum_high[:])

        gain256 = sb.tile([P, SLOTS], F32, name="gain256", tag="score_then_gain")
        nc.scalar.activation(gain256[:], gain[:], ACT.Copy, scale=256.0)

        inv_low = sb.tile([P, 1], F32, name="inv_low")
        nc.vector.reciprocal(inv_low[:], sum_low[:])
        avoided = sb.tile([P, SLOTS], F32, name="avoided")
        nc.vector.tensor_scalar(avoided[:], p_low[:], inv_low[:], averse_col[:], ALU.mult, ALU.mult)
        inv_high = sb.tile([P, 1], F32, name="inv_high")
        nc.vector.reciprocal(inv_high[:], sum_high[:])
        weight = sb.tile([P, SLOTS], F32, name="weight")
        nc.vector.scalar_tensor_tensor(weight[:], p_high[:], inv_high[:], avoided[:], ALU.mult, ALU.subtract)

        nc.vector.tensor_tensor(placed[:].indirect(place_list[:]), weight[:], gain256[:], ALU.mult)

        for c in range(T // STORE_COLS):
            cols = slice(c * STORE_COLS, (c + 1) * STORE_COLS)
            nc.vector.tensor_tensor(result[:, cols], placed[:, cols], result[:, cols], ALU.add)
            queue = nc.sync if c % 2 == 0 else nc.scalar
            queue.dma_start(out=out[:, cols], in_=result[:, cols])
